import numpy as np
import ml_dtypes


def mxq(x, axis, fmt="e4m3"):
    dtype, down = {"e4m3": (ml_dtypes.float8_e4m3fn, 7), "e5m2": (ml_dtypes.float8_e5m2, 14)}[fmt]
    v = np.moveaxis(np.asarray(x, np.float32).astype(ml_dtypes.bfloat16).astype(np.float64), axis, -1)
    blocks = v.reshape(v.shape[:-1] + (-1, 32))
    amax = np.abs(blocks).max(-1, keepdims=True)
    byte = np.maximum(np.where(amax > 0, np.frexp(amax)[1] - 1 + 127, 0) - down, 1)
    scale = np.exp2(byte - 127.0)
    codes = (blocks / scale).astype(np.float32).astype(dtype).astype(np.float64)
    return np.moveaxis((codes * scale).reshape(v.shape), -1, axis)


WIDE = False


def mx_kscale(k):
    if not WIDE:
        return np.ones(k)
    levels = np.array([18, -18])
    if k % 512:
        return np.exp2(np.random.permutation(np.resize(levels, k // 32))).repeat(32)
    a = np.empty((k // 512, 16))
    for p in range(k // 512):
        a[p, :8] = np.random.permutation(np.resize(levels, 8))
        for g in range(8):
            far = levels[np.abs(levels - a[p, g]) >= 10]
            a[p, g + 8] = far[np.random.randint(len(far))]
    return np.exp2(a.ravel()).repeat(32)


def f64(x):
    return np.asarray(x).astype(np.float64)


def striped(idx):
    return np.tile(np.asarray(idx).reshape(-1, 16).T, (8, 1)).astype(np.uint16)


def unstriped(offs):
    return offs[:16].T.reshape(-1).astype(np.int64)


B, N, T, D, R, TU = 2, 512, 2048, 512, 512, 2048


def setup_inputs():
    n = np.random.standard_normal
    idx = np.random.permutation(T)[:B * N]
    uidx = np.random.permutation(TU)[:B * R]
    s = mx_kscale(D)[:, None]
    z = np.ones(TU)
    z[uidx] = mx_kscale(B * R)
    u = np.ones(T)
    u[idx] = mx_kscale(B * N)
    r = np.random.uniform(0.5, 2.0, T) * u
    ur = np.random.uniform(0.5, 2.0, TU) * z
    return {
        "uT": (n((D, TU)) * s / ur).astype(np.float32),
        "vT": (n((D, T)) * (0.50 / np.sqrt(D)) / s / r).astype(np.float32),
        "y": np.exp(n((B, R, N))).astype(np.float32),
        "us": ur[uidx].reshape(B, R, 1).astype(np.float32),
        "ts": np.tile(r, (128, 1)).astype(np.float32),
        "offs": striped(idx),
        "uoffs": striped(uidx),
    }


def reference(uT, vT, y, us, ts, offs, uoffs):
    idx = unstriped(offs)
    pick = lambda x: x[:, idx].reshape(x.shape[0], B, N).transpose(1, 0, 2)
    uidx = unstriped(uoffs)
    w = pick(f64(vT))
    x = f64(uT)[:, uidx].reshape(D, B, R).transpose(1, 0, 2)
    a = mxq(x, 1, "e4m3").transpose(0, 2, 1) @ mxq(w, 1, "e4m3")
    sc = f64(us) * pick(f64(ts))[:, :1, :]
    a = a * sc
    g = (np.exp(a) - f64(y))
    h = sc * g
    dv = mxq(x, 2, "e4m3") @ mxq(h, 1, "e5m2")
    gv = np.zeros((D, T))
    gv[:, idx] = dv.transpose(1, 0, 2).reshape(D, B * N)
    du = mxq(w, 2, "e4m3") @ mxq(h, 2, "e5m2").transpose(0, 2, 1)
    gu = np.zeros((D, TU))
    gu[:, uidx] = du.transpose(1, 0, 2).reshape(D, B * R)
    return gv, gu

@@ -1,0 +1,275 @@
+from contextlib import ExitStack
+
+import concourse.mybir as mybir
+from concourse.masks import make_identity
+
+B, N, T, D = 2, 512, 2048, 512
+P = 128
+FLOPS = 3 * 2 * B * N * N * D
+BYTES = 4 * (4 * D * T + B * N * N + B * N + T) + 2 * 2 * P * (B * N // 16)
+
+F32 = mybir.dt.float32
+BF16 = mybir.dt.bfloat16
+U32 = mybir.dt.uint32
+U16 = mybir.dt.uint16
+U8 = mybir.dt.uint8
+E4 = mybir.dt.float8_e4m3fn_x4
+E5 = mybir.dt.float8_e5m2_x4
+MULT = mybir.AluOpType.mult
+ADD = mybir.AluOpType.add
+SUB = mybir.AluOpType.subtract
+COPY = mybir.ActivationFunctionType.Copy
+EXP = mybir.ActivationFunctionType.Exp
+
+G1_POOL = False
+SCALAR_SCATTER = False
+WARM = True
+
+
+def tile_attend_gmf_poi_vu_kernel(tc, uT, vT, y, us, ts, offs, uoffs, out_0, out_1):
+    nc = tc.nc
+    with ExitStack() as ctx:
+        keep = ctx.enter_context(tc.tile_pool(name="keep", bufs=1))
+        ring = ctx.enter_context(tc.tile_pool(name="ring", bufs=5))
+        turn = ctx.enter_context(tc.tile_pool(name="turn", bufs=3))
+        work = ctx.enter_context(tc.tile_pool(name="work", bufs=4))
+        ps_a = ctx.enter_context(tc.psum_pool(name="ps_a", bufs=3))
+        ps_o = ctx.enter_context(tc.psum_pool(name="ps_o", bufs=2))
+        ps_t = ctx.enter_context(tc.psum_pool(name="ps_t", bufs=3))
+
+        v_list = keep.tile([P, 64], U16, name="v_list")
+        u_list = keep.tile([P, 64], U16, name="u_list")
+        ident = keep.tile([P, P], F32, name="ident")
+        make_identity(nc, ident[:])
+
+        if WARM:
+            warm = keep.tile([P, 16], F32, name="warm")
+            nc.vector.memset(warm[:, 0:8], 0.0)
+            nc.scalar.activation(warm[:, 8:9], warm[:, 0:1], EXP)
+
+        ts_win = ring.tile([P, T], F32, name="ts_win", tag="ring", align_bytes=64)
+        nc.vector.memset(ts_win[:], 0.0)
+        nc.scalar.dma_start(ts_win[0:1, :], ts[0:1, :])
+        us_sb = keep.tile([P, B, 4], F32, name="us_sb")
+        nc.scalar.dma_start(us_sb[:], us.rearrange("b (s t) o -> s b (t o)", t=4))
+
+        tables = {"u": uT.rearrange("(p u e) c -> p u e c", u=2, e=2), "v": vT.rearrange("(p u e) c -> p u e c", u=2, e=2)}
+        lists = {"u": u_list, "v": v_list}
+        pairs = {}
+        for tab in ("u", "v"):
+            for u in range(2):
+                pairs[tab, u] = keep.tile([P, T, 2], BF16, name="pair_%s%d" % (tab, u), align_bytes=64)
+        gath = {tab: keep.tile([P, 2, 2 * B * N], BF16, name="gath_" + tab, align_bytes=64) for tab in ("u", "v")}
+
+        stage = {}
+        first = True
+        for tab in ("u", "v"):
+            for u in range(2):
+                for h in range(2):
+                    st = ring.tile([P, 2, 1024], F32, name="st_%s%d%d" % (tab, u, h), tag="ring", align_bytes=64)
+                    stage[tab, u, h] = st
+                    src = tables[tab][:, u, :, 1024 * h : 1024 * (h + 1)]
+                    if (tab, u) == ("v", 1):
+                        for q in range(2):
+                            nc.sync.dma_start(st[:, :, 512 * q : 512 * (q + 1)], src[:, :, 512 * q : 512 * (q + 1)])
+                    else:
+                        nc.sync.dma_start(st[:], src)
+                    if first:
+                        nc.sync.dma_start(v_list[:], offs)
+                        nc.sync.dma_start(u_list[:], uoffs)
+                        first = False
+        y_sb = []
+        for b in range(B):
+            yt = ring.tile([P, 4, N], F32, name="y%d" % b, tag="ring", align_bytes=64)
+            nc.sync.dma_start(yt[:], y[b].rearrange("(s t) i -> s t i", t=4))
+            y_sb.append(yt)
+
+        def cast(tab, u, h, c0, c1, eng):
+            dst = pairs[tab, u][:, 1024 * h + c0 : 1024 * h + c1, :]
+            src = stage[tab, u, h][:, :, c0:c1].rearrange("p e c -> p c e")
+            if eng == "V":
+                nc.vector.tensor_copy(dst, src)
+            else:
+                nc.scalar.activation(dst, src, COPY)
+
+        def gather(tab, u, b0, b1):
+            win = pairs[tab, u][:].rearrange("p c e -> p (c e)").bitcast(U32)
+            dst = gath[tab][:, u, :].bitcast(U32)[:, N * b0 : N * b1]
+            nc.vector.tensor_copy(dst, win.indirect(lists[tab][:, 32 * b0 : 32 * b1]))
+
+        def quant(src, name, fmt):
+            codes = keep.tile([P, N], U32, name="c_" + name, align_bytes=64)
+            scales = keep.tile([P, N], U8, name="s_" + name, align_bytes=64)
+            nc.vector.quantize_mx(out=codes[:].bitcast(fmt), scales=scales[:], in_=src[:])
+            return codes, scales, fmt
+
+        def mm(out, lhs, blk, rhs):
+            cols = slice(P * blk, P * (blk + 1))
+            nc.tensor.matmul_mx(out=out, lhsT=lhs[0][:, cols].bitcast(lhs[2]), lhsT_scale=lhs[1][:, cols],
+                                rhs=rhs[0][:].bitcast(rhs[2]), rhs_scale=rhs[1][:], start=True, stop=True)
+
+        def weave(tab, b, eng):
+            q = keep.tile([P, 4 * N], BF16, name="q_%s%d" % (tab, b), align_bytes=64)
+            src = gath[tab][:, :, 2 * N * b : 2 * N * (b + 1)]
+            if tab == "u":
+                dst_v = q[:].rearrange("p (t s u e) -> p s t u e", t=4, u=2, e=2)
+                src_v = src.rearrange("p u (s t e) -> p s t u e", t=4, e=2)
+            else:
+                dst_v = q[:].rearrange("p (c u e) -> p c u e", u=2, e=2)
+                src_v = src.rearrange("p u (c e) -> p c u e", e=2)
+            if eng == "V":
+                nc.vector.tensor_copy(dst_v, src_v)
+            else:
+                nc.scalar.copy(dst_v, src_v)
+            return q
+
+        def turn_half(dst, u, words):
+            bank = ps_t.tile([P, 4, P], F32, name="bank", tag="bank")
+            for t in range(4):
+                nc.tensor.transpose(bank[:, t, :], words(t), ident[:])
+            nc.scalar.copy(dst[:, 1024 * u : 1024 * (u + 1)].rearrange("q (e p t) -> q e p t", e=2, t=4),
+                           bank[:].rearrange("q t p -> q (t p)").bitcast(BF16).rearrange("q (t p e) -> q e p t", t=4, e=2))
+
+        def x_words(q, u):
+            return lambda t: q[:].bitcast(F32)[:, 256 * t + u : 256 * (t + 1) : 2]
+
+        def w_words(b, u):
+            return lambda t: gath["v"][:, u, :].bitcast(F32)[:, N * b + t : N * (b + 1) : 4]
+
+        ts_row = turn.tile([P, B * N], F32, name="ts_row", tag="turn", align_bytes=64)
+        nc.vector.tensor_copy(ts_row[:], ts_win[:].indirect(v_list[:]))
+
+        cast("u", 0, 0, 0, 1024, "S")
+        cast("u", 0, 1, 0, 1024, "S")
+        gather("u", 0, 0, 2)
+        cast("u", 1, 0, 0, 1024, "S")
+        cast("u", 1, 1, 0, 513, "S")
+        cast("u", 1, 1, 513, 1024, "V")
+        gather("u", 1, 0, 2)
+        cast("v", 0, 0, 0, 1024, "S")
+        cast("v", 0, 1, 0, 1024, "V")
+        cast("v", 1, 0, 0, 512, "S")
+        cast("v", 1, 0, 512, 1024, "S")
+        cast("v", 1, 1, 0, 512, "S")
+        cast("v", 1, 1, 512, 704, "S")
+        cast("v", 1, 1, 704, 1024, "V")
+        gather("v", 0, 0, 1)
+        gather("v", 1, 0, 1)
+        qw0 = weave("v", 0, "V")
+        qx0 = weave("u", 0, "V")
+        xd0 = quant(qx0, "xd0", E4)
+        wd0 = quant(qw0, "wd0", E4)
+
+        ts_col = keep.tile([P, 8], F32, name="ts_col")
+        ts_all = keep.tile([P, B * N], F32, name="ts_all")
+        for b in range(B):
+            bank = ps_t.tile([P, 4, P], F32, name="bank", tag="bank")
+            for k in range(4):
+                nc.tensor.transpose(bank[:, k, :], ts_row[:, N * b + P * k : N * b + P * (k + 1)], ident[:])
+            nc.scalar.copy(ts_col[:, 4 * b : 4 * (b + 1)], bank[:, :, 0])
+        for b in range(B):
+            bank = ps_t.tile([P, 4, P], F32, name="bank", tag="bank")
+            for k in range(4):
+                nc.tensor.transpose(bank[:, k, :], ts_col[:, 4 * b + k : 4 * b + k + 1].to_broadcast([P, P]), ident[:])
+            nc.scalar.copy(ts_all[:, N * b : N * (b + 1)], bank[:].rearrange("p k c -> p (k c)"))
+
+        def elementwise(b, xd, wd, pool):
+            h = keep.tile([P, 4, N], BF16, name="h%d" % b, align_bytes=64)
+            ht = turn.tile([P, 4 * N], BF16, name="ht%d" % b, tag="turn", align_bytes=64)
+            tsb = ts_all[:, N * b : N * (b + 1)]
+            if pool:
+                sc = keep.tile([P, 4, N], F32, name="sc%d" % b)
+            for t in range(4):
+                a = ps_a.tile([P, N], F32, name="a", tag="a")
+                mm(a[:], xd, t, wd)
+                usc = us_sb[:, b, t : t + 1]
+                e = work.tile([P, N], F32, name="e", tag="e")
+                yt = y_sb[b][:, t, :]
+                if pool:
+                    nc.scalar.activation(e[:], a[:], COPY, scale=usc)
+                    nc.gpsimd.tensor_tensor(e[:], e[:], tsb, MULT)
+                    nc.scalar.activation(e[:], e[:], EXP)
+                    nc.scalar.activation(sc[:, t, :], tsb, COPY, scale=usc)
+                    nc.gpsimd.tensor_tensor(yt, e[:], yt, SUB)
+                    nc.gpsimd.tensor_tensor(h[:, t, :], yt, sc[:, t, :], MULT)
+                else:
+                    nc.vector.tensor_tensor(e[:], a[:], tsb, MULT)
+                    nc.scalar.activation(e[:], e[:], EXP, scale=usc)
+                    nc.vector.tensor_tensor(yt, e[:], yt, SUB)
+                    nc.vector.scalar_tensor_tensor(h[:, t, :], yt, usc, tsb, MULT, MULT)
+                if t % 2 == 1:
+                    bank = ps_t.tile([P, 2, 2, P], F32, name="bank", tag="bank")
+                    for j in range(2):
+                        for u in range(2):
+                            nc.tensor.transpose(bank[:, j, u, :], h[:, t - 1 + j, :].bitcast(F32)[:, u:256:2], ident[:])
+                    nc.scalar.copy(ht[:].bitcast(F32).rearrange("q (s t u) -> q s t u", t=4, u=2)[:, :, t - 1 : t + 1, :],
+                                   bank[:].rearrange("q j u s -> q s j u"))
+            return h, ht
+
+        def weave_h(h, b):
+            hq = turn.tile([P, 4 * N], BF16, name="hq%d" % b, tag="turn", align_bytes=64)
+            nc.scalar.copy(hq[:].rearrange("p (c j t) -> p c t j", j=4, t=4), h[:].rearrange("p t (c j) -> p c t j", j=4))
+            return hq
+
+        def turned(name, words):
+            dst = turn.tile([P, 4 * N], BF16, name=name, tag="turn", align_bytes=64)
+            for u in range(2):
+                turn_half(dst, u, words(u))
+            return dst
+
+        def product(lhs, blk, rhs, dst=None):
+            acc = ps_o.tile([P, N], F32, name="acc", tag="acc")
+            mm(acc[:], lhs, blk, rhs)
+            if dst is None:
+                res = work.tile([P, N], F32, name="res", tag="res")
+                dst = res[:]
+            nc.scalar.copy(dst, acc[:])
+            return dst
+
+        def scatter(win, tab, b, src):
+            if SCALAR_SCATTER and tab == "v":
+                for k in range(2):
+                    nc.scalar.activation(win[:].indirect(lists[tab][:, 32 * b + 16 * k : 32 * b + 16 * (k + 1)]), src[:, 256 * k : 256 * (k + 1)], COPY)
+            else:
+                nc.vector.tensor_copy(win[:].indirect(lists[tab][:, 32 * b : 32 * (b + 1)]), src)
+
+        out_v = out_0.rearrange("(p t) c -> p t c", t=4)
+        out_u = out_1.rearrange("(p t) c -> p t c", t=4)
+        win_u = [keep.tile([P, T], F32, name="win_u%d" % t) for t in range(4)]
+        win_v = [keep.tile([P, T], F32, name="win_v%d" % t) for t in range(2)]
+
+        h0, ht0 = elementwise(0, xd0, wd0, False)
+        wt0 = quant(turned("wt0", lambda u: w_words(0, u)), "wt0", E4)
+        htq0 = quant(ht0, "ht0", E5)
+        for w in win_u + win_v:
+            nc.gpsimd.memset(w[:], 0.0)
+        gather("v", 0, 1, 2)
+        gather("v", 1, 1, 2)
+        qx1 = weave("u", 1, "S")
+        qw1 = weave("v", 1, "S")
+        xd1 = quant(qx1, "xd1", E4)
+        wd1 = quant(qw1, "wd1", E4)
+        du0 = [product(wt0, t, htq0) for t in range(2)]
+        xt0 = quant(turned("xt0", lambda u: x_words(qx0, u)), "xt0", E4)
+        hq0 = quant(weave_h(h0, 0), "hq0", E5)
+        h1, ht1 = elementwise(1, xd1, wd1, G1_POOL)
+        wt1 = quant(turned("wt1", lambda u: w_words(1, u)), "wt1", E4)
+        htq1 = quant(ht1, "ht1", E5)
+        xt1 = quant(turned("xt1", lambda u: x_words(qx1, u)), "xt1", E4)
+        hq1 = quant(weave_h(h1, 1), "hq1", E5)
+        for t in range(4):
+            scatter(win_u[t], "u", 0, du0[t] if t < 2 else product(wt0, t, htq0))
+        for t in range(2):
+            scatter(win_v[t], "v", 0, product(xt0, t, hq0))
+        for kind, t in (("u", 0), ("u", 1), ("v", 0), ("v", 1), ("u", 2), ("u", 3)):
+            if kind == "u":
+                scatter(win_u[t], "u", 1, product(wt1, t, htq1))
+                nc.sync.dma_start(out_u[:, t, :], win_u[t][:])
+            else:
+                scatter(win_v[t], "v", 1, product(xt1, t, hq1))
+                nc.sync.dma_start(out_v[:, t, :], win_v[t][:])
+        late = ring.tile([P, 4, N], F32, name="late", tag="ring", align_bytes=64)
+        for t in range(2, 4):
+            scatter(win_v[t - 2], "v", 0, product(xt0, t, hq0, late[:, 2 * (t - 2), :]))
+            scatter(win_v[t - 2], "v", 1, product(xt1, t, hq1, late[:, 2 * (t - 2) + 1, :]))
+            nc.sync.dma_start(out_v[:, t, :], win_v[t - 2][:])

@@ -21,84 +21,106 @@ SUB = mybir.AluOpType.subtract
 COPY = mybir.ActivationFunctionType.Copy
 EXP = mybir.ActivationFunctionType.Exp
 
-G1_POOL = False
-SCALAR_SCATTER = False
-WARM = True
+MODE = "PE"
 
 
 def tile_attend_gmf_poi_vu_kernel(tc, uT, vT, y, us, ts, offs, uoffs, out_0, out_1):
     nc = tc.nc
     with ExitStack() as ctx:
         keep = ctx.enter_context(tc.tile_pool(name="keep", bufs=1))
-        ring = ctx.enter_context(tc.tile_pool(name="ring", bufs=5))
-        turn = ctx.enter_context(tc.tile_pool(name="turn", bufs=3))
+        turn = ctx.enter_context(tc.tile_pool(name="turn", bufs=2))
         work = ctx.enter_context(tc.tile_pool(name="work", bufs=4))
-        ps_a = ctx.enter_context(tc.psum_pool(name="ps_a", bufs=3))
-        ps_o = ctx.enter_context(tc.psum_pool(name="ps_o", bufs=2))
-        ps_t = ctx.enter_context(tc.psum_pool(name="ps_t", bufs=3))
+        ps_a = ctx.enter_context(tc.psum_pool(name="ps_a", bufs=4))
+        ps_t = ctx.enter_context(tc.psum_pool(name="ps_t", bufs=1))
+
+        def held(shape, dtype, name, tag=None):
+            return keep.tile(shape, dtype, name=name, tag=tag or name, align_bytes=64)
 
         v_list = keep.tile([P, 64], U16, name="v_list")
         u_list = keep.tile([P, 64], U16, name="u_list")
         ident = keep.tile([P, P], F32, name="ident")
-        make_identity(nc, ident[:])
-
-        if WARM:
-            warm = keep.tile([P, 16], F32, name="warm")
-            nc.vector.memset(warm[:, 0:8], 0.0)
-            nc.scalar.activation(warm[:, 8:9], warm[:, 0:1], EXP)
-
-        ts_win = ring.tile([P, T], F32, name="ts_win", tag="ring", align_bytes=64)
+        warm = keep.tile([P, 16], F32, name="warm")
+        nc.gpsimd.memset(warm[:, 0:8], 0.0)
+        nc.scalar.activation(warm[:, 8:9], warm[:, 0:1], EXP)
+        ts_win = held([P, T], F32, "ts_win")
         nc.vector.memset(ts_win[:], 0.0)
-        nc.scalar.dma_start(ts_win[0:1, :], ts[0:1, :])
+        make_identity(nc, ident[:])
         us_sb = keep.tile([P, B, 4], F32, name="us_sb")
         nc.scalar.dma_start(us_sb[:], us.rearrange("b (s t) o -> s b (t o)", t=4))
+        nc.scalar.dma_start(ts_win[0:1, :], ts[0:1, :])
+        wins = []
 
         tables = {"u": uT.rearrange("(p u e) c -> p u e c", u=2, e=2), "v": vT.rearrange("(p u e) c -> p u e c", u=2, e=2)}
         lists = {"u": u_list, "v": v_list}
         pairs = {}
         for tab in ("u", "v"):
             for u in range(2):
-                pairs[tab, u] = keep.tile([P, T, 2], BF16, name="pair_%s%d" % (tab, u), align_bytes=64)
-        gath = {tab: keep.tile([P, 2, 2 * B * N], BF16, name="gath_" + tab, align_bytes=64) for tab in ("u", "v")}
+                pairs[tab, u] = held([P, T, 2], BF16, "pair_%s%d" % (tab, u))
+        gath = {"u": held([P, 4 * 2 * N], BF16, "gath_u"), "v": held([P, 3 * 2 * N], BF16, "gath_v")}
+        place = {("u", 0, 0): 0, ("u", 0, 1): 1, ("u", 1, 0): 2, ("u", 1, 1): 3, ("v", 0, 0): 0, ("v", 0, 1): 1, ("v", 1, 0): 2, ("v", 1, 1): 2}
 
         stage = {}
         first = True
         for tab in ("u", "v"):
             for u in range(2):
                 for h in range(2):
-                    st = ring.tile([P, 2, 1024], F32, name="st_%s%d%d" % (tab, u, h), tag="ring", align_bytes=64)
+                    st = held([P, 2, 1024], F32, "st_%s%d%d" % (tab, u, h), "r%d" % (len(stage) % 5))
                     stage[tab, u, h] = st
                     src = tables[tab][:, u, :, 1024 * h : 1024 * (h + 1)]
                     if (tab, u) == ("v", 1):
                         for q in range(2):
-                            nc.sync.dma_start(st[:, :, 512 * q : 512 * (q + 1)], src[:, :, 512 * q : 512 * (q + 1)])
+                            nc.sync.dma_start(st[:, q, :].rearrange("p (e c) -> p e c", e=2), src[:, :, 512 * q : 512 * (q + 1)])
                     else:
                         nc.sync.dma_start(st[:], src)
                     if first:
                         nc.sync.dma_start(v_list[:], offs)
                         nc.sync.dma_start(u_list[:], uoffs)
                         first = False
-        y_sb = []
-        for b in range(B):
-            yt = ring.tile([P, 4, N], F32, name="y%d" % b, tag="ring", align_bytes=64)
+
+        spare = [held([P, 4, N], F32, "spare%d" % k, "r%d" % (k + 1)) for k in range(2)]
+        ring_wins = [held([P, T], F32, "win6", "r0")]
+
+        def load_y(b, tag):
+            yt = held([P, 4, N], F32, "y%d" % b, tag)
             nc.sync.dma_start(yt[:], y[b].rearrange("(s t) i -> s t i", t=4))
-            y_sb.append(yt)
+            return yt
+
+        def late_window(k, tag):
+            w = held([P, T], F32, "win%d" % k, tag) if k != 6 else ring_wins[0]
+            if k == 0:
+                nc.vector.memset(w[:], 0.0)
+            elif k < 6:
+                nc.gpsimd.memset(w[:], 0.0)
+            else:
+                for j in range(2):
+                    nc.gpsimd.memset(w[:, T // 2 * j : T // 2 * (j + 1)], 0.0)
+            wins.append(w)
 
         def cast(tab, u, h, c0, c1, eng):
             dst = pairs[tab, u][:, 1024 * h + c0 : 1024 * h + c1, :]
-            src = stage[tab, u, h][:, :, c0:c1].rearrange("p e c -> p c e")
+            if (tab, u) == ("v", 1):
+                q = c0 // 512
+                src = stage[tab, u, h][:, q, :].rearrange("p (e c) -> p c e", e=2)[:, c0 - 512 * q : c1 - 512 * q, :]
+            else:
+                src = stage[tab, u, h][:, :, c0:c1].rearrange("p e c -> p c e")
             if eng == "V":
                 nc.vector.tensor_copy(dst, src)
             else:
                 nc.scalar.activation(dst, src, COPY)
 
+        def both(tab, u, h, c0, c1, c2):
+            if c1 > c0:
+                cast(tab, u, h, c0, c1, "S")
+            if c2 > c1:
+                cast(tab, u, h, c1, c2, "V")
+
         def gather(tab, u, b0, b1):
             win = pairs[tab, u][:].rearrange("p c e -> p (c e)").bitcast(U32)
-            dst = gath[tab][:, u, :].bitcast(U32)[:, N * b0 : N * b1]
+            dst = gath[tab][:].bitcast(U32)[:, N * place[tab, u, b0] : N * (place[tab, u, b0] + b1 - b0)]
             nc.vector.tensor_copy(dst, win.indirect(lists[tab][:, 32 * b0 : 32 * b1]))
 
-        def quant(src, name, fmt):
-            codes = keep.tile([P, N], U32, name="c_" + name, align_bytes=64)
+        def quant(src, name, fmt, slot=None):
+            codes = held([P, N], U32, "c_" + name, slot)
             scales = keep.tile([P, N], U8, name="s_" + name, align_bytes=64)
             nc.vector.quantize_mx(out=codes[:].bitcast(fmt), scales=scales[:], in_=src[:])
             return codes, scales, fmt
@@ -108,10 +130,11 @@ def tile_attend_gmf_poi_vu_kernel(tc, uT, vT, y, us, ts, offs, uoffs, out_0, out
             nc.tensor.matmul_mx(out=out, lhsT=lhs[0][:, cols].bitcast(lhs[2]), lhsT_scale=lhs[1][:, cols],
                                 rhs=rhs[0][:].bitcast(rhs[2]), rhs_scale=rhs[1][:], start=True, stop=True)
 
-        def weave(tab, b, eng):
-            q = keep.tile([P, 4 * N], BF16, name="q_%s%d" % (tab, b), align_bytes=64)
-            src = gath[tab][:, :, 2 * N * b : 2 * N * (b + 1)]
-            if tab == "u":
+        def weave(tab, b, eng, fours, tag=None):
+            q = held([P, 4 * N], BF16, "q_%s%d" % (tab, b), tag)
+            lo, hi = place[tab, 0, b], place[tab, 1, b]
+            src = gath[tab][:].rearrange("p (g c) -> p g c", c=2 * N)[:, lo : hi + 1 : hi - lo, :]
+            if fours:
                 dst_v = q[:].rearrange("p (t s u e) -> p s t u e", t=4, u=2, e=2)
                 src_v = src.rearrange("p u (s t e) -> p s t u e", t=4, e=2)
             else:
@@ -123,153 +146,223 @@ def tile_attend_gmf_poi_vu_kernel(tc, uT, vT, y, us, ts, offs, uoffs, out_0, out
                 nc.scalar.copy(dst_v, src_v)
             return q
 
-        def turn_half(dst, u, words):
-            bank = ps_t.tile([P, 4, P], F32, name="bank", tag="bank")
-            for t in range(4):
-                nc.tensor.transpose(bank[:, t, :], words(t), ident[:])
-            nc.scalar.copy(dst[:, 1024 * u : 1024 * (u + 1)].rearrange("q (e p t) -> q e p t", e=2, t=4),
-                           bank[:].rearrange("q t p -> q (t p)").bitcast(BF16).rearrange("q (t p e) -> q e p t", t=4, e=2))
+        def new_bank(tag):
+            if tag == "a":
+                return ps_a.tile([P, 4, P], F32, name="bank", tag="a")
+            return ps_t.tile([P, 4, P], F32, name="bank", tag="bank" + tag)
 
-        def x_words(q, u):
-            return lambda t: q[:].bitcast(F32)[:, 256 * t + u : 256 * (t + 1) : 2]
+        def turned(name, words, tags, slot=None):
+            dst = held([P, 4 * N], BF16, name, slot) if slot else turn.tile([P, 4 * N], BF16, name=name, tag="turn", align_bytes=64)
+            for u in range(len(tags)):
+                turn_half(dst, words, u, tags[u])
+            return dst
 
-        def w_words(b, u):
-            return lambda t: gath["v"][:, u, :].bitcast(F32)[:, N * b + t : N * (b + 1) : 4]
+        def turn_half(dst, words, u, tag):
+            if True:
+                bank = new_bank(tag)
+                for t in range(4):
+                    nc.tensor.transpose(bank[:, t, :], words(u, t), ident[:])
+                nc.scalar.copy(dst[:, 1024 * u : 1024 * (u + 1)].rearrange("q (e p t) -> q e p t", e=2, t=4),
+                               bank[:].rearrange("q t p -> q (t p)").bitcast(BF16).rearrange("q (t p e) -> q e p t", t=4, e=2))
 
-        ts_row = turn.tile([P, B * N], F32, name="ts_row", tag="turn", align_bytes=64)
-        nc.vector.tensor_copy(ts_row[:], ts_win[:].indirect(v_list[:]))
+        def q_words(q):
+            return lambda u, t: q[:].bitcast(F32)[:, 256 * t + u : 256 * (t + 1) : 2]
 
-        cast("u", 0, 0, 0, 1024, "S")
-        cast("u", 0, 1, 0, 1024, "S")
-        gather("u", 0, 0, 2)
-        cast("u", 1, 0, 0, 1024, "S")
-        cast("u", 1, 1, 0, 513, "S")
-        cast("u", 1, 1, 513, 1024, "V")
-        gather("u", 1, 0, 2)
-        cast("v", 0, 0, 0, 1024, "S")
-        cast("v", 0, 1, 0, 1024, "V")
-        cast("v", 1, 0, 0, 512, "S")
-        cast("v", 1, 0, 512, 1024, "S")
-        cast("v", 1, 1, 0, 512, "S")
-        cast("v", 1, 1, 512, 704, "S")
-        cast("v", 1, 1, 704, 1024, "V")
-        gather("v", 0, 0, 1)
-        gather("v", 1, 0, 1)
-        qw0 = weave("v", 0, "V")
-        qx0 = weave("u", 0, "V")
-        xd0 = quant(qx0, "xd0", E4)
-        wd0 = quant(qw0, "wd0", E4)
+        def g_words(b):
+            return lambda u, t: gath["v"][:].bitcast(F32)[:, N * place["v", u, b] + t : N * (place["v", u, b] + 1) : 4]
 
-        ts_col = keep.tile([P, 8], F32, name="ts_col")
-        ts_all = keep.tile([P, B * N], F32, name="ts_all")
-        for b in range(B):
-            bank = ps_t.tile([P, 4, P], F32, name="bank", tag="bank")
-            for k in range(4):
-                nc.tensor.transpose(bank[:, k, :], ts_row[:, N * b + P * k : N * b + P * (k + 1)], ident[:])
-            nc.scalar.copy(ts_col[:, 4 * b : 4 * (b + 1)], bank[:, :, 0])
-        for b in range(B):
-            bank = ps_t.tile([P, 4, P], F32, name="bank", tag="bank")
-            for k in range(4):
-                nc.tensor.transpose(bank[:, k, :], ts_col[:, 4 * b + k : 4 * b + k + 1].to_broadcast([P, P]), ident[:])
-            nc.scalar.copy(ts_all[:, N * b : N * (b + 1)], bank[:].rearrange("p k c -> p (k c)"))
+        def turn_h(h, dst, t):
+            bank = new_bank("A" if t == 1 else "B")
+            for j in range(2):
+                for u in range(2):
+                    nc.tensor.transpose(bank[:, 2 * j + u, :], h[:, t - 1 + j, :].bitcast(F32)[:, u:256:2], ident[:])
+            nc.scalar.copy(dst[:].bitcast(F32).rearrange("q (s t u) -> q s t u", t=4, u=2)[:, :, t - 1 : t + 1, :],
+                           bank[:].rearrange("q (j u) s -> q s j u", u=2))
 
-        def elementwise(b, xd, wd, pool):
+        def elementwise(b, xd, wd, yb, pool):
             h = keep.tile([P, 4, N], BF16, name="h%d" % b, align_bytes=64)
-            ht = turn.tile([P, 4 * N], BF16, name="ht%d" % b, tag="turn", align_bytes=64)
+            ht = held([P, 4 * N], BF16, "ht%d" % b, "hx")
             tsb = ts_all[:, N * b : N * (b + 1)]
+            es = []
             if pool:
-                sc = keep.tile([P, 4, N], F32, name="sc%d" % b)
+                sc = spare[0]
+                e4 = held([P, 4, N], F32, "e4", "r3")
             for t in range(4):
                 a = ps_a.tile([P, N], F32, name="a", tag="a")
                 mm(a[:], xd, t, wd)
                 usc = us_sb[:, b, t : t + 1]
-                e = work.tile([P, N], F32, name="e", tag="e")
-                yt = y_sb[b][:, t, :]
+                yt = yb[:, t, :]
                 if pool:
-                    nc.scalar.activation(e[:], a[:], COPY, scale=usc)
-                    nc.gpsimd.tensor_tensor(e[:], e[:], tsb, MULT)
-                    nc.scalar.activation(e[:], e[:], EXP)
-                    nc.scalar.activation(sc[:, t, :], tsb, COPY, scale=usc)
-                    nc.gpsimd.tensor_tensor(yt, e[:], yt, SUB)
+                    e = e4[:, t, :]
+                    nc.scalar.activation(e, a[:], COPY, scale=usc)
+                    nc.gpsimd.tensor_tensor(e, e, tsb, MULT)
+                    nc.scalar.activation(e, e, EXP)
+                    nc.gpsimd.tensor_scalar(sc[:, t, :], tsb, usc, 0.0, MULT, ADD)
+                    nc.gpsimd.tensor_tensor(yt, e, yt, SUB)
                     nc.gpsimd.tensor_tensor(h[:, t, :], yt, sc[:, t, :], MULT)
+                    if t % 2 == 1:
+                        turn_h(h, ht, t)
                 else:
-                    nc.vector.tensor_tensor(e[:], a[:], tsb, MULT)
-                    nc.scalar.activation(e[:], e[:], EXP, scale=usc)
-                    nc.vector.tensor_tensor(yt, e[:], yt, SUB)
-                    nc.vector.scalar_tensor_tensor(h[:, t, :], yt, usc, tsb, MULT, MULT)
+                    e = held([P, N], F32, "e%d%d" % (b, t), "e%d" % t) if b == 0 else spare[1][:, t, :]
+                    arg = held([P, N], F32, "arg", "arg") if (b, t) == (0, 3) else e
+                    nc.vector.tensor_tensor(arg[:], a[:], tsb, MULT)
+                    nc.scalar.activation(e[:], arg[:], EXP, scale=usc)
+                    es.append(e)
+            for t in range(len(es)):
+                yt = yb[:, t, :]
+                nc.vector.tensor_tensor(yt, es[t][:], yt, SUB)
                 if t % 2 == 1:
-                    bank = ps_t.tile([P, 2, 2, P], F32, name="bank", tag="bank")
-                    for j in range(2):
-                        for u in range(2):
-                            nc.tensor.transpose(bank[:, j, u, :], h[:, t - 1 + j, :].bitcast(F32)[:, u:256:2], ident[:])
-                    nc.scalar.copy(ht[:].bitcast(F32).rearrange("q (s t u) -> q s t u", t=4, u=2)[:, :, t - 1 : t + 1, :],
-                                   bank[:].rearrange("q j u s -> q s j u"))
+                    for j in (t - 1, t):
+                        nc.vector.scalar_tensor_tensor(h[:, j, :], yb[:, j, :], us_sb[:, b, j : j + 1], tsb, MULT, MULT)
+                    turn_h(h, ht, t)
             return h, ht
 
+        def elementwise_turned(b, xd, wd, yb, between):
+            h = keep.tile([P, 4, N], BF16, name="h%d" % b, align_bytes=64)
+            bt, e4 = spare
+            ny = held([P, 4, N], F32, "ny", "r3")
+            nus = keep.tile([P, 4], F32, name="nus")
+            nc.gpsimd.tensor_scalar(nus[:], us_sb[:, b, :], -1.0, 0.0, MULT, ADD)
+            for t in range(4):
+                a = ps_a.tile([P, N], F32, name="a", tag="a")
+                mm(a[:], wd, t, xd)
+                nc.scalar.activation(bt[:, t, :], a[:], COPY, scale=ts_col[:, 4 * b + t : 4 * b + t + 1])
+            between()
+            for t in range(4):
+                bank = new_bank("AB"[t % 2])
+                for k in range(4):
+                    nc.tensor.transpose(bank[:, k, :], bt[:, k, P * t : P * (t + 1)], ident[:])
+                usc = us_sb[:, b, t : t + 1]
+                nc.scalar.activation(e4[:, t, :], bank[:].rearrange("p k s -> p (k s)"), EXP, scale=usc)
+                nc.scalar.activation(e4[:, t, :], e4[:, t, :], COPY, scale=usc)
+                nc.scalar.activation(ny[:, t, :].rearrange("p (k s) -> p s k", k=4), yb[:, t, :].rearrange("p (s k) -> p s k", k=4), COPY, scale=nus[:, t : t + 1])
+            hx = held([P, 4 * N], BF16, "ht%d" % b, "hx")
+            for k in range(4):
+                bank = new_bank("CD"[k % 2])
+                for t in range(4):
+                    nc.tensor.matmul(bank[:, t, :], e4[:, t, P * k : P * (k + 1)], ident[:], start=True, stop=False, is_transpose=True)
+                    nc.tensor.matmul(bank[:, t, :], ny[:, t, P * k : P * (k + 1)], ident[:], start=False, stop=True, is_transpose=True)
+                nc.scalar.activation(h[:, k, :].rearrange("p (s t) -> p s t", t=4), bank[:].rearrange("p t s -> p s t"), COPY,
+                                     scale=ts_col[:, 4 * b + k : 4 * b + k + 1])
+                if k % 2 == 1:
+                    turn_h(h, hx, k)
+            return h, hx
+
         def weave_h(h, b):
-            hq = turn.tile([P, 4 * N], BF16, name="hq%d" % b, tag="turn", align_bytes=64)
-            nc.scalar.copy(hq[:].rearrange("p (c j t) -> p c t j", j=4, t=4), h[:].rearrange("p t (c j) -> p c t j", j=4))
+            hq = held([P, 4 * N], BF16, "hq%d" % b, "hx")
+            for k in range(4):
+                nc.scalar.copy(hq[:, N * k : N * (k + 1)].rearrange("p (c j t) -> p c t j", j=4, t=4),
+                               h[:, :, P * k : P * (k + 1)].rearrange("p t (c j) -> p c t j", j=4))
             return hq
 
-        def turned(name, words):
-            dst = turn.tile([P, 4 * N], BF16, name=name, tag="turn", align_bytes=64)
-            for u in range(2):
-                turn_half(dst, u, words(u))
-            return dst
-
-        def product(lhs, blk, rhs, dst=None):
-            acc = ps_o.tile([P, N], F32, name="acc", tag="acc")
+        def product(lhs, blk, rhs):
+            acc = ps_a.tile([P, N], F32, name="acc", tag="a")
             mm(acc[:], lhs, blk, rhs)
-            if dst is None:
-                res = work.tile([P, N], F32, name="res", tag="res")
-                dst = res[:]
-            nc.scalar.copy(dst, acc[:])
-            return dst
+            res = work.tile([P, N], F32, name="res", tag="res")
+            nc.scalar.copy(res[:], acc[:])
+            return res
 
         def scatter(win, tab, b, src):
-            if SCALAR_SCATTER and tab == "v":
-                for k in range(2):
-                    nc.scalar.activation(win[:].indirect(lists[tab][:, 32 * b + 16 * k : 32 * b + 16 * (k + 1)]), src[:, 256 * k : 256 * (k + 1)], COPY)
-            else:
-                nc.vector.tensor_copy(win[:].indirect(lists[tab][:, 32 * b : 32 * (b + 1)]), src)
+            nc.vector.tensor_copy(win[:].indirect(lists[tab][:, 32 * b : 32 * (b + 1)]), src[:])
 
         out_v = out_0.rearrange("(p t) c -> p t c", t=4)
         out_u = out_1.rearrange("(p t) c -> p t c", t=4)
-        win_u = [keep.tile([P, T], F32, name="win_u%d" % t) for t in range(4)]
-        win_v = [keep.tile([P, T], F32, name="win_v%d" % t) for t in range(2)]
 
-        h0, ht0 = elementwise(0, xd0, wd0, False)
-        wt0 = quant(turned("wt0", lambda u: w_words(0, u)), "wt0", E4)
-        htq0 = quant(ht0, "ht0", E5)
-        for w in win_u + win_v:
-            nc.gpsimd.memset(w[:], 0.0)
-        gather("v", 0, 1, 2)
-        gather("v", 1, 1, 2)
-        qx1 = weave("u", 1, "S")
-        qw1 = weave("v", 1, "S")
+        ts_row = turn.tile([P, B * N], F32, name="ts_row", tag="turn", align_bytes=64)
+        nc.vector.tensor_copy(ts_row[:], ts_win[:].indirect(v_list[:]))
+        for k in range(5):
+            late_window(k, None)
+        late_window(5, "ts_win")
+
+        ts_col = keep.tile([P, 8], F32, name="ts_col")
+        ts_all = keep.tile([P, B * N], F32, name="ts_all")
+        for b in range(B):
+            bank = new_bank("AB"[b])
+            for k in range(4):
+                if MODE == "PE" and b == 1:
+                    nc.tensor.transpose(bank[:, k, :], ts_row[:, N * b + k : N * (b + 1) : 4], ident[:])
+                else:
+                    nc.tensor.transpose(bank[:, k, :], ts_row[:, N * b + P * k : N * b + P * (k + 1)], ident[:])
+            nc.scalar.copy(ts_col[:, 4 * b : 4 * (b + 1)], bank[:, :, 0])
+        for b in range(1 if MODE == "PE" else 2):
+            bank = new_bank("AB"[b])
+            for k in range(4):
+                nc.tensor.transpose(bank[:, k, :], ts_col[:, 4 * b + k : 4 * b + k + 1].to_broadcast([P, P]), ident[:])
+            nc.scalar.copy(ts_all[:, N * b : N * (b + 1)], bank[:].rearrange("p k c -> p (k c)"))
+
+        both("u", 0, 0, 0, 1024, 1024)
+        both("u", 0, 1, 0, 1024, 1024)
+        gather("u", 0, 0, 2)
+        both("u", 1, 0, 0, 1024, 1024)
+        both("u", 1, 1, 0, 513, 1024)
+        gather("u", 1, 0, 2)
+        y0 = load_y(0, "r3")
+        qx0 = weave("u", 0, "V", True)
+        qx1 = weave("u", 1, "V", True)
+        y1 = load_y(1, "r4")
+        xd0 = quant(qx0, "xd0", E4)
+        both("v", 0, 0, 0, 1024, 1024)
+        both("v", 0, 1, 0, 512, 1024)
         xd1 = quant(qx1, "xd1", E4)
+        gather("v", 0, 0, 1)
+        gather("v", 0, 1, 2)
+        late_window(6, None)
+        both("v", 1, 0, 0, 512, 512)
+        both("v", 1, 0, 512, 1024, 1024)
+        both("v", 1, 1, 0, 512, 512)
+        both("v", 1, 1, 512, 769, 1024)
+        gather("v", 1, 0, 1)
+        qw0 = weave("v", 0, "V", False)
+        wd0 = quant(qw0, "wd0", E4)
+
+        wt0s = turned("wt0", g_words(0), "AB")
+        h0, ht0 = elementwise(0, xd0, wd0, y0, False)
+        xt0s = turned("xt0", q_words(qx0), "CD")
+        xt1s = turned("xt1", q_words(qx1), "aa", "arg")
+        wt0 = quant(wt0s, "wt0", E4, "e1")
+        htq0 = quant(ht0, "ht0", E5)
+        du0 = [product(wt0, t, htq0) for t in range(4)]
+        gather("v", 1, 1, 2)
+        late_window(7, "q_v0")
+        win_u, win_v = wins[:4], wins[4:]
+        qw1 = weave("v", 1, "V", MODE == "PE", "e3")
         wd1 = quant(qw1, "wd1", E4)
-        du0 = [product(wt0, t, htq0) for t in range(2)]
-        xt0 = quant(turned("xt0", lambda u: x_words(qx0, u)), "xt0", E4)
-        hq0 = quant(weave_h(h0, 0), "hq0", E5)
-        h1, ht1 = elementwise(1, xd1, wd1, G1_POOL)
-        wt1 = quant(turned("wt1", lambda u: w_words(1, u)), "wt1", E4)
-        htq1 = quant(ht1, "ht1", E5)
-        xt1 = quant(turned("xt1", lambda u: x_words(qx1, u)), "xt1", E4)
-        hq1 = quant(weave_h(h1, 1), "hq1", E5)
-        for t in range(4):
-            scatter(win_u[t], "u", 0, du0[t] if t < 2 else product(wt0, t, htq0))
-        for t in range(2):
-            scatter(win_v[t], "v", 0, product(xt0, t, hq0))
-        for kind, t in (("u", 0), ("u", 1), ("v", 0), ("v", 1), ("u", 2), ("u", 3)):
-            if kind == "u":
-                scatter(win_u[t], "u", 1, product(wt1, t, htq1))
-                nc.sync.dma_start(out_u[:, t, :], win_u[t][:])
-            else:
-                scatter(win_v[t], "v", 1, product(xt1, t, hq1))
-                nc.sync.dma_start(out_v[:, t, :], win_v[t][:])
-        late = ring.tile([P, 4, N], F32, name="late", tag="ring", align_bytes=64)
+        dv0 = []
+
+        def group0_rest():
+            hq0s = weave_h(h0, 0)
+            for t in range(2):
+                scatter(win_u[t], "u", 0, du0[t])
+            hq0 = quant(hq0s, "hq0", E5)
+            dv0.extend(product(xt0, t, hq0) for t in range(4))
+
+        xt0 = quant(xt0s, "xt0", E4, "e2")
+        if MODE == "PE":
+            h1, hx1 = elementwise_turned(1, xd1, wd1, y1, group0_rest)
+            a1s = xt1s
+            b1s = turned("wt1", q_words(qw1), "CD")
+        else:
+            group0_rest()
+            h1, hx1 = elementwise(1, xd1, wd1, y1, MODE == "G")
+            a1s = turned("wt1", g_words(1), "CD")
+            b1s = xt1s
         for t in range(2, 4):
-            scatter(win_v[t - 2], "v", 0, product(xt0, t, hq0, late[:, 2 * (t - 2), :]))
-            scatter(win_v[t - 2], "v", 1, product(xt1, t, hq1, late[:, 2 * (t - 2) + 1, :]))
-            nc.sync.dma_start(out_v[:, t, :], win_v[t - 2][:])
+            scatter(win_u[t], "u", 0, du0[t])
+        for t in range(3):
+            scatter(win_v[t], "v", 0, dv0[t])
+        a1 = quant(a1s, "a1", E4)
+        ha1 = quant(hx1, "ha1", E5)
+        first1 = [product(a1, t, ha1) for t in range(4)]
+        hb1s = weave_h(h1, 1)
+        first_kind, second_kind = "vu" if MODE == "PE" else "uv"
+        scatter(win_v[3], "v", 0, dv0[3])
+        sides = {"u": (win_u, out_u), "v": (win_v, out_v)}
+        for t in range(4):
+            if t == 2:
+                b1 = quant(b1s, "b1", E4)
+                hb1 = quant(hb1s, "hb1", E5)
+            scatter(sides[first_kind][0][t], first_kind, 1, first1[t])
+            nc.sync.dma_start(sides[first_kind][1][:, t, :], sides[first_kind][0][t][:])
+        for t in range(4):
+            scatter(sides[second_kind][0][t], second_kind, 1, product(b1, t, hb1))
+            nc.sync.dma_start(sides[second_kind][1][:, t, :], sides[second_kind][0][t][:])

@@ -21,98 +21,67 @@ SUB = mybir.AluOpType.subtract
 COPY = mybir.ActivationFunctionType.Copy
 EXP = mybir.ActivationFunctionType.Exp
 
-MODE = "PE"
-
 
 def tile_attend_gmf_poi_vu_kernel(tc, uT, vT, y, us, ts, offs, uoffs, out_0, out_1):
     nc = tc.nc
     with ExitStack() as ctx:
         keep = ctx.enter_context(tc.tile_pool(name="keep", bufs=1))
         turn = ctx.enter_context(tc.tile_pool(name="turn", bufs=2))
-        work = ctx.enter_context(tc.tile_pool(name="work", bufs=4))
-        ps_a = ctx.enter_context(tc.psum_pool(name="ps_a", bufs=4))
-        ps_t = ctx.enter_context(tc.psum_pool(name="ps_t", bufs=1))
+        ps_ring = ctx.enter_context(tc.psum_pool(name="ps_ring", bufs=4))
+        ps_named = ctx.enter_context(tc.psum_pool(name="ps_named", bufs=1))
 
-        def held(shape, dtype, name, tag=None):
-            return keep.tile(shape, dtype, name=name, tag=tag or name, align_bytes=64)
+        def held(shape, dtype, name, slot=None):
+            return keep.tile(shape, dtype, name=name, tag=slot or name, align_bytes=64)
 
-        v_list = keep.tile([P, 64], U16, name="v_list")
-        u_list = keep.tile([P, 64], U16, name="u_list")
+        def new_bank(which):
+            if which == "r":
+                return ps_ring.tile([P, 4, P], F32, name="bank", tag="ring")
+            return ps_named.tile([P, 4, P], F32, name="bank", tag="bank" + which)
+
+        lists = {"v": keep.tile([P, 64], U16, name="v_list"), "u": keep.tile([P, 64], U16, name="u_list")}
         ident = keep.tile([P, P], F32, name="ident")
-        warm = keep.tile([P, 16], F32, name="warm")
-        nc.gpsimd.memset(warm[:, 0:8], 0.0)
-        nc.scalar.activation(warm[:, 8:9], warm[:, 0:1], EXP)
         ts_win = held([P, T], F32, "ts_win")
-        nc.vector.memset(ts_win[:], 0.0)
+        nc.gpsimd.memset(ts_win[:], 0.0)
         make_identity(nc, ident[:])
         us_sb = keep.tile([P, B, 4], F32, name="us_sb")
         nc.scalar.dma_start(us_sb[:], us.rearrange("b (s t) o -> s b (t o)", t=4))
         nc.scalar.dma_start(ts_win[0:1, :], ts[0:1, :])
-        wins = []
+        nus = keep.tile([P, 4], F32, name="nus")
+        nc.scalar.activation(nus[:], us_sb[:, 1, :], COPY, scale=-1.0)
 
         tables = {"u": uT.rearrange("(p u e) c -> p u e c", u=2, e=2), "v": vT.rearrange("(p u e) c -> p u e c", u=2, e=2)}
-        lists = {"u": u_list, "v": v_list}
-        pairs = {}
-        for tab in ("u", "v"):
-            for u in range(2):
-                pairs[tab, u] = held([P, T, 2], BF16, "pair_%s%d" % (tab, u))
+        pairs = {(tab, u): held([P, T, 2], BF16, "pair_%s%d" % (tab, u)) for tab in "uv" for u in range(2)}
         gath = {"u": held([P, 4 * 2 * N], BF16, "gath_u"), "v": held([P, 3 * 2 * N], BF16, "gath_v")}
         place = {("u", 0, 0): 0, ("u", 0, 1): 1, ("u", 1, 0): 2, ("u", 1, 1): 3, ("v", 0, 0): 0, ("v", 0, 1): 1, ("v", 1, 0): 2, ("v", 1, 1): 2}
 
-        stage = {}
-        first = True
-        for tab in ("u", "v"):
-            for u in range(2):
-                for h in range(2):
-                    st = held([P, 2, 1024], F32, "st_%s%d%d" % (tab, u, h), "r%d" % (len(stage) % 5))
-                    stage[tab, u, h] = st
-                    src = tables[tab][:, u, :, 1024 * h : 1024 * (h + 1)]
-                    if (tab, u) == ("v", 1):
-                        for q in range(2):
-                            nc.sync.dma_start(st[:, q, :].rearrange("p (e c) -> p e c", e=2), src[:, :, 512 * q : 512 * (q + 1)])
-                    else:
-                        nc.sync.dma_start(st[:], src)
-                    if first:
-                        nc.sync.dma_start(v_list[:], offs)
-                        nc.sync.dma_start(u_list[:], uoffs)
-                        first = False
-
-        spare = [held([P, 4, N], F32, "spare%d" % k, "r%d" % (k + 1)) for k in range(2)]
-        ring_wins = [held([P, T], F32, "win6", "r0")]
-
-        def load_y(b, tag):
-            yt = held([P, 4, N], F32, "y%d" % b, tag)
-            nc.sync.dma_start(yt[:], y[b].rearrange("(s t) i -> s t i", t=4))
-            return yt
-
-        def late_window(k, tag):
-            w = held([P, T], F32, "win%d" % k, tag) if k != 6 else ring_wins[0]
+        chunks = [("u", 0, 0, 1024, "s0"), ("u", 0, 1024, 1024, "s1"), ("u", 1, 0, 1024, "s2"), ("u", 1, 1024, 1024, "s3"),
+                  ("v", 0, 0, 1024, "s4"), ("v", 0, 1024, 1024, "s0"), ("v", 1, 0, 1024, "s1"),
+                  ("v", 1, 1024, 512, "s2"), ("v", 1, 1536, 512, "s4")]
+        stage = []
+        for k, (tab, u, c0, width, slot) in enumerate(chunks):
+            stage.append(held([P, 2, width], F32, "chunk%d" % k, slot))
+            nc.sync.dma_start(stage[k][:], tables[tab][:, u, :, c0 : c0 + width])
             if k == 0:
-                nc.vector.memset(w[:], 0.0)
-            elif k < 6:
-                nc.gpsimd.memset(w[:], 0.0)
-            else:
-                for j in range(2):
-                    nc.gpsimd.memset(w[:, T // 2 * j : T // 2 * (j + 1)], 0.0)
-            wins.append(w)
+                nc.sync.dma_start(lists["v"][:], offs)
+                nc.sync.dma_start(lists["u"][:], uoffs)
+        y_sb = []
+        for b, slot in enumerate(("s0", "s1")):
+            y_sb.append(held([P, 4, N], F32, "y%d" % b, slot))
+            nc.sync.dma_start(y_sb[b][:], y[b].rearrange("(s t) i -> s t i", t=4))
 
-        def cast(tab, u, h, c0, c1, eng):
-            dst = pairs[tab, u][:, 1024 * h + c0 : 1024 * h + c1, :]
-            if (tab, u) == ("v", 1):
-                q = c0 // 512
-                src = stage[tab, u, h][:, q, :].rearrange("p (e c) -> p c e", e=2)[:, c0 - 512 * q : c1 - 512 * q, :]
-            else:
-                src = stage[tab, u, h][:, :, c0:c1].rearrange("p e c -> p c e")
-            if eng == "V":
-                nc.vector.tensor_copy(dst, src)
-            else:
-                nc.scalar.activation(dst, src, COPY)
+        def window(k, slot=None):
+            w = held([P, T], F32, "win%d" % k, slot)
+            nc.gpsimd.memset(w[:], 0.0)
+            return w
 
-        def both(tab, u, h, c0, c1, c2):
-            if c1 > c0:
-                cast(tab, u, h, c0, c1, "S")
-            if c2 > c1:
-                cast(tab, u, h, c1, c2, "V")
+        def cast(k, split):
+            tab, u, c0, width, slot = chunks[k]
+            dst = pairs[tab, u][:, c0 : c0 + width, :]
+            src = stage[k][:].rearrange("p e c -> p c e")
+            if split > 0:
+                nc.scalar.activation(dst[:, :split, :], src[:, :split, :], COPY)
+            if split < width:
+                nc.vector.tensor_copy(dst[:, split:, :], src[:, split:, :])
 
         def gather(tab, u, b0, b1):
             win = pairs[tab, u][:].rearrange("p c e -> p (c e)").bitcast(U32)
@@ -121,7 +90,7 @@ def tile_attend_gmf_poi_vu_kernel(tc, uT, vT, y, us, ts, offs, uoffs, out_0, out
 
         def quant(src, name, fmt, slot=None):
             codes = held([P, N], U32, "c_" + name, slot)
-            scales = keep.tile([P, N], U8, name="s_" + name, align_bytes=64)
+            scales = held([P, N], U8, "s_" + name)
             nc.vector.quantize_mx(out=codes[:].bitcast(fmt), scales=scales[:], in_=src[:])
             return codes, scales, fmt
 
@@ -130,46 +99,34 @@ def tile_attend_gmf_poi_vu_kernel(tc, uT, vT, y, us, ts, offs, uoffs, out_0, out
             nc.tensor.matmul_mx(out=out, lhsT=lhs[0][:, cols].bitcast(lhs[2]), lhsT_scale=lhs[1][:, cols],
                                 rhs=rhs[0][:].bitcast(rhs[2]), rhs_scale=rhs[1][:], start=True, stop=True)
 
-        def weave(tab, b, eng, fours, tag=None):
-            q = held([P, 4 * N], BF16, "q_%s%d" % (tab, b), tag)
+        def weave(tab, b, fours, slot=None):
+            q = held([P, 4 * N], BF16, "q_%s%d" % (tab, b), slot)
             lo, hi = place[tab, 0, b], place[tab, 1, b]
             src = gath[tab][:].rearrange("p (g c) -> p g c", c=2 * N)[:, lo : hi + 1 : hi - lo, :]
             if fours:
-                dst_v = q[:].rearrange("p (t s u e) -> p s t u e", t=4, u=2, e=2)
-                src_v = src.rearrange("p u (s t e) -> p s t u e", t=4, e=2)
+                nc.vector.tensor_copy(q[:].rearrange("p (t s u e) -> p s t u e", t=4, u=2, e=2), src.rearrange("p u (s t e) -> p s t u e", t=4, e=2))
             else:
-                dst_v = q[:].rearrange("p (c u e) -> p c u e", u=2, e=2)
-                src_v = src.rearrange("p u (c e) -> p c u e", e=2)
-            if eng == "V":
-                nc.vector.tensor_copy(dst_v, src_v)
-            else:
-                nc.scalar.copy(dst_v, src_v)
+                nc.vector.tensor_copy(q[:].rearrange("p (c u e) -> p c u e", u=2, e=2), src.rearrange("p u (c e) -> p c u e", e=2))
             return q
 
-        def new_bank(tag):
-            if tag == "a":
-                return ps_a.tile([P, 4, P], F32, name="bank", tag="a")
-            return ps_t.tile([P, 4, P], F32, name="bank", tag="bank" + tag)
-
-        def turned(name, words, tags, slot=None):
+        def turned(name, words, banks, slot=None):
             dst = held([P, 4 * N], BF16, name, slot) if slot else turn.tile([P, 4 * N], BF16, name=name, tag="turn", align_bytes=64)
-            for u in range(len(tags)):
-                turn_half(dst, words, u, tags[u])
+            for u, which in enumerate(banks):
+                turn_pair(dst, words, u, which)
             return dst
 
-        def turn_half(dst, words, u, tag):
-            if True:
-                bank = new_bank(tag)
-                for t in range(4):
-                    nc.tensor.transpose(bank[:, t, :], words(u, t), ident[:])
-                nc.scalar.copy(dst[:, 1024 * u : 1024 * (u + 1)].rearrange("q (e p t) -> q e p t", e=2, t=4),
-                               bank[:].rearrange("q t p -> q (t p)").bitcast(BF16).rearrange("q (t p e) -> q e p t", t=4, e=2))
+        def turn_pair(dst, words, u, which):
+            bank = new_bank(which)
+            for t in range(4):
+                nc.tensor.transpose(bank[:, t, :], words(u, t), ident[:])
+            nc.scalar.copy(dst[:, 1024 * u : 1024 * (u + 1)].rearrange("q (e p t) -> q e p t", e=2, t=4),
+                           bank[:].rearrange("q t p -> q (t p)").bitcast(BF16).rearrange("q (t p e) -> q e p t", t=4, e=2))
 
-        def q_words(q):
+        def woven_words(q):
             return lambda u, t: q[:].bitcast(F32)[:, 256 * t + u : 256 * (t + 1) : 2]
 
-        def g_words(b):
-            return lambda u, t: gath["v"][:].bitcast(F32)[:, N * place["v", u, b] + t : N * (place["v", u, b] + 1) : 4]
+        def gathered_words(u, t):
+            return gath["v"][:].bitcast(F32)[:, N * place["v", u, 0] + t : N * (place["v", u, 0] + 1) : 4]
 
         def turn_h(h, dst, t):
             bank = new_bank("A" if t == 1 else "B")
@@ -179,190 +136,153 @@ def tile_attend_gmf_poi_vu_kernel(tc, uT, vT, y, us, ts, offs, uoffs, out_0, out
             nc.scalar.copy(dst[:].bitcast(F32).rearrange("q (s t u) -> q s t u", t=4, u=2)[:, :, t - 1 : t + 1, :],
                            bank[:].rearrange("q (j u) s -> q s j u", u=2))
 
-        def elementwise(b, xd, wd, yb, pool):
-            h = keep.tile([P, 4, N], BF16, name="h%d" % b, align_bytes=64)
-            ht = held([P, 4 * N], BF16, "ht%d" % b, "hx")
-            tsb = ts_all[:, N * b : N * (b + 1)]
-            es = []
-            if pool:
-                sc = spare[0]
-                e4 = held([P, 4, N], F32, "e4", "r3")
-            for t in range(4):
-                a = ps_a.tile([P, N], F32, name="a", tag="a")
-                mm(a[:], xd, t, wd)
-                usc = us_sb[:, b, t : t + 1]
-                yt = yb[:, t, :]
-                if pool:
-                    e = e4[:, t, :]
-                    nc.scalar.activation(e, a[:], COPY, scale=usc)
-                    nc.gpsimd.tensor_tensor(e, e, tsb, MULT)
-                    nc.scalar.activation(e, e, EXP)
-                    nc.gpsimd.tensor_scalar(sc[:, t, :], tsb, usc, 0.0, MULT, ADD)
-                    nc.gpsimd.tensor_tensor(yt, e, yt, SUB)
-                    nc.gpsimd.tensor_tensor(h[:, t, :], yt, sc[:, t, :], MULT)
-                    if t % 2 == 1:
-                        turn_h(h, ht, t)
-                else:
-                    e = held([P, N], F32, "e%d%d" % (b, t), "e%d" % t) if b == 0 else spare[1][:, t, :]
-                    arg = held([P, N], F32, "arg", "arg") if (b, t) == (0, 3) else e
-                    nc.vector.tensor_tensor(arg[:], a[:], tsb, MULT)
-                    nc.scalar.activation(e[:], arg[:], EXP, scale=usc)
-                    es.append(e)
-            for t in range(len(es)):
-                yt = yb[:, t, :]
-                nc.vector.tensor_tensor(yt, es[t][:], yt, SUB)
-                if t % 2 == 1:
-                    for j in (t - 1, t):
-                        nc.vector.scalar_tensor_tensor(h[:, j, :], yb[:, j, :], us_sb[:, b, j : j + 1], tsb, MULT, MULT)
-                    turn_h(h, ht, t)
-            return h, ht
-
-        def elementwise_turned(b, xd, wd, yb, between):
-            h = keep.tile([P, 4, N], BF16, name="h%d" % b, align_bytes=64)
-            bt, e4 = spare
-            ny = held([P, 4, N], F32, "ny", "r3")
-            nus = keep.tile([P, 4], F32, name="nus")
-            nc.gpsimd.tensor_scalar(nus[:], us_sb[:, b, :], -1.0, 0.0, MULT, ADD)
-            for t in range(4):
-                a = ps_a.tile([P, N], F32, name="a", tag="a")
-                mm(a[:], wd, t, xd)
-                nc.scalar.activation(bt[:, t, :], a[:], COPY, scale=ts_col[:, 4 * b + t : 4 * b + t + 1])
-            between()
-            for t in range(4):
-                bank = new_bank("AB"[t % 2])
-                for k in range(4):
-                    nc.tensor.transpose(bank[:, k, :], bt[:, k, P * t : P * (t + 1)], ident[:])
-                usc = us_sb[:, b, t : t + 1]
-                nc.scalar.activation(e4[:, t, :], bank[:].rearrange("p k s -> p (k s)"), EXP, scale=usc)
-                nc.scalar.activation(e4[:, t, :], e4[:, t, :], COPY, scale=usc)
-                nc.scalar.activation(ny[:, t, :].rearrange("p (k s) -> p s k", k=4), yb[:, t, :].rearrange("p (s k) -> p s k", k=4), COPY, scale=nus[:, t : t + 1])
-            hx = held([P, 4 * N], BF16, "ht%d" % b, "hx")
-            for k in range(4):
-                bank = new_bank("CD"[k % 2])
-                for t in range(4):
-                    nc.tensor.matmul(bank[:, t, :], e4[:, t, P * k : P * (k + 1)], ident[:], start=True, stop=False, is_transpose=True)
-                    nc.tensor.matmul(bank[:, t, :], ny[:, t, P * k : P * (k + 1)], ident[:], start=False, stop=True, is_transpose=True)
-                nc.scalar.activation(h[:, k, :].rearrange("p (s t) -> p s t", t=4), bank[:].rearrange("p t s -> p s t"), COPY,
-                                     scale=ts_col[:, 4 * b + k : 4 * b + k + 1])
-                if k % 2 == 1:
-                    turn_h(h, hx, k)
-            return h, hx
-
-        def weave_h(h, b):
-            hq = held([P, 4 * N], BF16, "hq%d" % b, "hx")
+        def weave_h(h, name):
+            hq = held([P, 4 * N], BF16, name, "hx")
             for k in range(4):
                 nc.scalar.copy(hq[:, N * k : N * (k + 1)].rearrange("p (c j t) -> p c t j", j=4, t=4),
                                h[:, :, P * k : P * (k + 1)].rearrange("p t (c j) -> p c t j", j=4))
             return hq
 
-        def product(lhs, blk, rhs):
-            acc = ps_a.tile([P, N], F32, name="acc", tag="a")
-            mm(acc[:], lhs, blk, rhs)
-            res = work.tile([P, N], F32, name="res", tag="res")
-            nc.scalar.copy(res[:], acc[:])
-            return res
+        def flat(bank):
+            return bank[:].rearrange("p k s -> p (k s)")
+
+        def product(res, lhs, blk, rhs, which="r"):
+            acc = new_bank(which)
+            mm(flat(acc), lhs, blk, rhs)
+            nc.scalar.copy(res[:, blk, :], flat(acc))
 
         def scatter(win, tab, b, src):
-            nc.vector.tensor_copy(win[:].indirect(lists[tab][:, 32 * b : 32 * (b + 1)]), src[:])
+            nc.vector.tensor_copy(win[:].indirect(lists[tab][:, 32 * b : 32 * (b + 1)]), src)
+
+        ts_row = turn.tile([P, B * N], F32, name="ts_row", tag="turn", align_bytes=64)
+        nc.vector.tensor_copy(ts_row[:], ts_win[:].indirect(lists["v"][:]))
+        win_u = [window(k) for k in range(4)]
+        win_v = [window(4)]
+
+        cast(0, 513)
+        cast(1, 1024)
+        gather("u", 0, 0, 2)
+        cast(2, 1024)
+        cast(3, 1024)
+        gather("u", 1, 0, 2)
+
+        ts_col = keep.tile([P, 8], F32, name="ts_col")
+        ts_all = keep.tile([P, N], F32, name="ts_all")
+        bank = new_bank("A")
+        for k in range(4):
+            nc.tensor.transpose(bank[:, k, :], ts_row[:, P * k : P * (k + 1)], ident[:])
+        nc.vector.tensor_copy(ts_col[:, 0:4], bank[:, :, 0])
+        bank = new_bank("B")
+        for k in range(4):
+            nc.tensor.transpose(bank[:, k, :], ts_row[:, N + k : 2 * N : 4], ident[:])
+        nc.vector.tensor_copy(ts_col[:, 4:8], bank[:, :, 0])
+        bank = new_bank("A")
+        for k in range(4):
+            nc.tensor.transpose(bank[:, k, :], ts_col[:, k : k + 1].to_broadcast([P, P]), ident[:])
+        nc.vector.tensor_copy(ts_all[:], flat(bank))
+
+        qx0 = weave("u", 0, True)
+        qx1 = weave("u", 1, True)
+        xd0 = quant(qx0, "xd0", E4)
+        xd1 = quant(qx1, "xd1", E4)
+        cast(4, 1024)
+        cast(5, 1024)
+        gather("v", 0, 0, 2)
+        cast(6, 1024)
+        cast(7, 512)
+        cast(8, 0)
+        gather("v", 1, 0, 1)
+        qw0 = weave("v", 0, False)
+        wd0 = quant(qw0, "wd0", E4)
+        wt0s = turned("wt0", gathered_words, "A")
+
+        h0 = held([P, 4, N], BF16, "h0")
+        ht0s = held([P, 4 * N], BF16, "ht0", "hx")
+        e0 = []
+        for t in range(4):
+            a = new_bank("r")
+            mm(flat(a), xd0, t, wd0)
+            e0.append(held([P, N], F32, "e%d" % t))
+            arg = held([P, N], F32, "arg") if t == 3 else e0[t]
+            nc.vector.tensor_tensor(arg[:], flat(a), ts_all[:], MULT)
+            nc.scalar.activation(e0[t][:], arg[:], EXP, scale=us_sb[:, 0, t : t + 1])
+        for t in range(4):
+            nc.vector.tensor_tensor(y_sb[0][:, t, :], e0[t][:], y_sb[0][:, t, :], SUB)
+            if t % 2 == 1:
+                for j in (t - 1, t):
+                    nc.vector.scalar_tensor_tensor(h0[:, j, :], y_sb[0][:, j, :], us_sb[:, 0, j : j + 1], ts_all[:], MULT, MULT)
+                turn_h(h0, ht0s, t)
+        turn_pair(wt0s, gathered_words, 1, "r")
+        xt0s = turned("xt0", woven_words(qx0), "CD")
+        xt1s = turned("xt1", woven_words(qx1), "rr", "arg")
+        wt0 = quant(wt0s, "wt0", E4, "e1")
+        ht0 = quant(ht0s, "ht0", E5)
+        du0 = held([P, 4, N], F32, "du0", "pair_u0")
+        product(du0, wt0, 0, ht0)
+        hq0s = weave_h(h0, "hq0")
+        for t in range(1, 4):
+            product(du0, wt0, t, ht0)
+        gather("v", 1, 1, 2)
+        win_v.extend(window(5 + k, slot) for k, slot in enumerate(("q_v0", "c_wd0", "e0")))
+        qw1 = weave("v", 1, True, "e3")
+        wd1 = quant(qw1, "wd1", E4)
+        xt0 = quant(xt0s, "xt0", E4, "e2")
+        xt1 = quant(xt1s, "xt1", E4)
+        hq0 = quant(hq0s, "hq0", E5)
+
+        h1 = held([P, 4, N], BF16, "h1")
+        bt = held([P, 4, N], F32, "bt", "s2")
+        e1 = held([P, 4, N], F32, "e_1", "s3")
+        ny = held([P, 4, N], F32, "ny", "s0")
+        for t in range(4):
+            a = new_bank("r")
+            mm(flat(a), wd1, t, xd1)
+            nc.scalar.activation(bt[:, t, :], flat(a), COPY, scale=ts_col[:, 4 + t : 5 + t])
+        dv0 = held([P, 4, N], F32, "dv0", "pair_u1")
+        for t in range(3):
+            product(dv0, xt0, t, hq0)
+        for t in range(4):
+            bank = new_bank("AB"[t % 2])
+            for k in range(4):
+                nc.tensor.transpose(bank[:, k, :], bt[:, k, P * t : P * (t + 1)], ident[:])
+            usc = us_sb[:, 1, t : t + 1]
+            nc.scalar.activation(e1[:, t, :], flat(bank), EXP, scale=usc)
+            nc.scalar.activation(e1[:, t, :], e1[:, t, :], COPY, scale=usc)
+            nc.scalar.activation(ny[:, t, :].rearrange("p (k s) -> p s k", k=4), y_sb[1][:, t, :].rearrange("p (s k) -> p s k", k=4), COPY, scale=nus[:, t : t + 1])
+        hq1s = held([P, 4 * N], BF16, "hq1", "hx")
+        for k in range(4):
+            bank = new_bank("CD"[k % 2])
+            for t in range(4):
+                nc.tensor.matmul(bank[:, t, :], e1[:, t, P * k : P * (k + 1)], ident[:], start=True, stop=False, is_transpose=True)
+                nc.tensor.matmul(bank[:, t, :], ny[:, t, P * k : P * (k + 1)], ident[:], start=False, stop=True, is_transpose=True)
+            nc.scalar.activation(h1[:, k, :].rearrange("p (s t) -> p s t", t=4), bank[:].rearrange("p t s -> p s t"), COPY,
+                                 scale=ts_col[:, 4 + k : 5 + k])
+            if k % 2 == 1:
+                turn_h(h1, hq1s, k)
+        hq1 = quant(hq1s, "hq1", E5)
+        product(dv0, xt0, 3, hq0, "B")
+        dv1 = held([P, 4, N], F32, "dv1", "pair_u0")
+        for t in range(2):
+            product(dv1, xt1, t, hq1)
+        ht1s = weave_h(h1, "ht1")
+        wt1s = turned("wt1", woven_words(qw1), "CD")
+        for t in range(2, 4):
+            product(dv1, xt1, t, hq1)
+        wt1 = quant(wt1s, "wt1", E4)
+        ht1 = quant(ht1s, "ht1", E5)
+        du1 = held([P, 4, N], F32, "du1", "pair_u1")
+        for t in range(4):
+            product(du1, wt1, t, ht1)
 
         out_v = out_0.rearrange("(p t) c -> p t c", t=4)
         out_u = out_1.rearrange("(p t) c -> p t c", t=4)
-
-        ts_row = turn.tile([P, B * N], F32, name="ts_row", tag="turn", align_bytes=64)
-        nc.vector.tensor_copy(ts_row[:], ts_win[:].indirect(v_list[:]))
-        for k in range(5):
-            late_window(k, None)
-        late_window(5, "ts_win")
-
-        ts_col = keep.tile([P, 8], F32, name="ts_col")
-        ts_all = keep.tile([P, B * N], F32, name="ts_all")
-        for b in range(B):
-            bank = new_bank("AB"[b])
-            for k in range(4):
-                if MODE == "PE" and b == 1:
-                    nc.tensor.transpose(bank[:, k, :], ts_row[:, N * b + k : N * (b + 1) : 4], ident[:])
-                else:
-                    nc.tensor.transpose(bank[:, k, :], ts_row[:, N * b + P * k : N * b + P * (k + 1)], ident[:])
-            nc.scalar.copy(ts_col[:, 4 * b : 4 * (b + 1)], bank[:, :, 0])
-        for b in range(1 if MODE == "PE" else 2):
-            bank = new_bank("AB"[b])
-            for k in range(4):
-                nc.tensor.transpose(bank[:, k, :], ts_col[:, 4 * b + k : 4 * b + k + 1].to_broadcast([P, P]), ident[:])
-            nc.scalar.copy(ts_all[:, N * b : N * (b + 1)], bank[:].rearrange("p k c -> p (k c)"))
-
-        both("u", 0, 0, 0, 1024, 1024)
-        both("u", 0, 1, 0, 1024, 1024)
-        gather("u", 0, 0, 2)
-        both("u", 1, 0, 0, 1024, 1024)
-        both("u", 1, 1, 0, 513, 1024)
-        gather("u", 1, 0, 2)
-        y0 = load_y(0, "r3")
-        qx0 = weave("u", 0, "V", True)
-        qx1 = weave("u", 1, "V", True)
-        y1 = load_y(1, "r4")
-        xd0 = quant(qx0, "xd0", E4)
-        both("v", 0, 0, 0, 1024, 1024)
-        both("v", 0, 1, 0, 512, 1024)
-        xd1 = quant(qx1, "xd1", E4)
-        gather("v", 0, 0, 1)
-        gather("v", 0, 1, 2)
-        late_window(6, None)
-        both("v", 1, 0, 0, 512, 512)
-        both("v", 1, 0, 512, 1024, 1024)
-        both("v", 1, 1, 0, 512, 512)
-        both("v", 1, 1, 512, 769, 1024)
-        gather("v", 1, 0, 1)
-        qw0 = weave("v", 0, "V", False)
-        wd0 = quant(qw0, "wd0", E4)
-
-        wt0s = turned("wt0", g_words(0), "AB")
-        h0, ht0 = elementwise(0, xd0, wd0, y0, False)
-        xt0s = turned("xt0", q_words(qx0), "CD")
-        xt1s = turned("xt1", q_words(qx1), "aa", "arg")
-        wt0 = quant(wt0s, "wt0", E4, "e1")
-        htq0 = quant(ht0, "ht0", E5)
-        du0 = [product(wt0, t, htq0) for t in range(4)]
-        gather("v", 1, 1, 2)
-        late_window(7, "q_v0")
-        win_u, win_v = wins[:4], wins[4:]
-        qw1 = weave("v", 1, "V", MODE == "PE", "e3")
-        wd1 = quant(qw1, "wd1", E4)
-        dv0 = []
-
-        def group0_rest():
-            hq0s = weave_h(h0, 0)
-            for t in range(2):
-                scatter(win_u[t], "u", 0, du0[t])
-            hq0 = quant(hq0s, "hq0", E5)
-            dv0.extend(product(xt0, t, hq0) for t in range(4))
-
-        xt0 = quant(xt0s, "xt0", E4, "e2")
-        if MODE == "PE":
-            h1, hx1 = elementwise_turned(1, xd1, wd1, y1, group0_rest)
-            a1s = xt1s
-            b1s = turned("wt1", q_words(qw1), "CD")
-        else:
-            group0_rest()
-            h1, hx1 = elementwise(1, xd1, wd1, y1, MODE == "G")
-            a1s = turned("wt1", g_words(1), "CD")
-            b1s = xt1s
-        for t in range(2, 4):
-            scatter(win_u[t], "u", 0, du0[t])
-        for t in range(3):
-            scatter(win_v[t], "v", 0, dv0[t])
-        a1 = quant(a1s, "a1", E4)
-        ha1 = quant(hx1, "ha1", E5)
-        first1 = [product(a1, t, ha1) for t in range(4)]
-        hb1s = weave_h(h1, 1)
-        first_kind, second_kind = "vu" if MODE == "PE" else "uv"
-        scatter(win_v[3], "v", 0, dv0[3])
-        sides = {"u": (win_u, out_u), "v": (win_v, out_v)}
         for t in range(4):
-            if t == 2:
-                b1 = quant(b1s, "b1", E4)
-                hb1 = quant(hb1s, "hb1", E5)
-            scatter(sides[first_kind][0][t], first_kind, 1, first1[t])
-            nc.sync.dma_start(sides[first_kind][1][:, t, :], sides[first_kind][0][t][:])
+            scatter(win_u[t], "u", 0, du0[:, t, :])
         for t in range(4):
-            scatter(sides[second_kind][0][t], second_kind, 1, product(b1, t, hb1))
-            nc.sync.dma_start(sides[second_kind][1][:, t, :], sides[second_kind][0][t][:])
+            scatter(win_v[t], "v", 0, dv0[:, t, :])
+        for t in range(4):
+            scatter(win_v[t], "v", 1, dv1[:, t, :])
+            nc.sync.dma_start(out_v[:, t, :], win_v[t][:])
+        for t in range(4):
+            scatter(win_u[t], "u", 1, du1[:, t, :])
+            nc.sync.dma_start(out_u[:, t, :], win_u[t][:])

from contextlib import ExitStack

import concourse.mybir as mybir
from concourse.masks import make_identity

B, N, T, D = 2, 512, 2048, 512
P = 128
FLOPS = 3 * 2 * B * N * N * D
BYTES = 4 * (4 * D * T + B * N * N + B * N + T) + 2 * 2 * P * (B * N // 16)

F32 = mybir.dt.float32
BF16 = mybir.dt.bfloat16
U32 = mybir.dt.uint32
U16 = mybir.dt.uint16
U8 = mybir.dt.uint8
E4 = mybir.dt.float8_e4m3fn_x4
E5 = mybir.dt.float8_e5m2_x4
MULT = mybir.AluOpType.mult
ADD = mybir.AluOpType.add
SUB = mybir.AluOpType.subtract
COPY = mybir.ActivationFunctionType.Copy
EXP = mybir.ActivationFunctionType.Exp


def tile_attend_gmf_poi_vu_kernel(tc, uT, vT, y, us, ts, offs, uoffs, out_0, out_1):
    nc = tc.nc
    with ExitStack() as ctx:
        keep = ctx.enter_context(tc.tile_pool(name="keep", bufs=1))
        turn = ctx.enter_context(tc.tile_pool(name="turn", bufs=2))
        ps_ring = ctx.enter_context(tc.psum_pool(name="ps_ring", bufs=4))
        ps_named = ctx.enter_context(tc.psum_pool(name="ps_named", bufs=1))

        def held(shape, dtype, name, slot=None):
            return keep.tile(shape, dtype, name=name, tag=slot or name, align_bytes=64)

        def new_bank(which):
            if which == "r":
                return ps_ring.tile([P, 4, P], F32, name="bank", tag="ring")
            return ps_named.tile([P, 4, P], F32, name="bank", tag="bank" + which)

        lists = {"v": keep.tile([P, 64], U16, name="v_list"), "u": keep.tile([P, 64], U16, name="u_list")}
        ident = keep.tile([P, P], F32, name="ident")
        ts_win = held([P, T], F32, "ts_win")
        nc.gpsimd.memset(ts_win[:], 0.0)
        make_identity(nc, ident[:])
        us_sb = keep.tile([P, B, 4], F32, name="us_sb")
        nc.scalar.dma_start(us_sb[:], us.rearrange("b (s t) o -> s b (t o)", t=4))
        nc.scalar.dma_start(ts_win[0:1, :], ts[0:1, :])
        nus = keep.tile([P, 4], F32, name="nus")
        nc.scalar.activation(nus[:], us_sb[:, 1, :], COPY, scale=-1.0)

        tables = {"u": uT.rearrange("(p u e) c -> p u e c", u=2, e=2), "v": vT.rearrange("(p u e) c -> p u e c", u=2, e=2)}
        pairs = {(tab, u): held([P, T, 2], BF16, "pair_%s%d" % (tab, u)) for tab in "uv" for u in range(2)}
        gath = {"u": held([P, 4 * 2 * N], BF16, "gath_u"), "v": held([P, 3 * 2 * N], BF16, "gath_v")}
        place = {("u", 0, 0): 0, ("u", 0, 1): 1, ("u", 1, 0): 2, ("u", 1, 1): 3, ("v", 0, 0): 0, ("v", 0, 1): 1, ("v", 1, 0): 2, ("v", 1, 1): 2}

        chunks = [("u", 0, 0, 1024, "s0"), ("u", 0, 1024, 1024, "s1"), ("u", 1, 0, 1024, "s2"), ("u", 1, 1024, 1024, "s3"),
                  ("v", 0, 0, 1024, "s4"), ("v", 0, 1024, 1024, "s0"), ("v", 1, 0, 1024, "s1"),
                  ("v", 1, 1024, 512, "s2"), ("v", 1, 1536, 512, "s4")]
        stage = []
        for k, (tab, u, c0, width, slot) in enumerate(chunks):
            stage.append(held([P, 2, width], F32, "chunk%d" % k, slot))
            nc.sync.dma_start(stage[k][:], tables[tab][:, u, :, c0 : c0 + width])
            if k == 0:
                nc.sync.dma_start(lists["v"][:], offs)
                nc.sync.dma_start(lists["u"][:], uoffs)
        y_sb = []
        for b, slot in enumerate(("s0", "s1")):
            y_sb.append(held([P, 4, N], F32, "y%d" % b, slot))
            nc.sync.dma_start(y_sb[b][:], y[b].rearrange("(s t) i -> s t i", t=4))

        def window(k, slot=None):
            w = held([P, T], F32, "win%d" % k, slot)
            nc.gpsimd.memset(w[:], 0.0)
            return w

        def cast(k, split):
            tab, u, c0, width, slot = chunks[k]
            dst = pairs[tab, u][:, c0 : c0 + width, :]
            src = stage[k][:].rearrange("p e c -> p c e")
            if split > 0:
                nc.scalar.activation(dst[:, :split, :], src[:, :split, :], COPY)
            if split < width:
                nc.vector.tensor_copy(dst[:, split:, :], src[:, split:, :])

        def gather(tab, u, b0, b1):
            win = pairs[tab, u][:].rearrange("p c e -> p (c e)").bitcast(U32)
            dst = gath[tab][:].bitcast(U32)[:, N * place[tab, u, b0] : N * (place[tab, u, b0] + b1 - b0)]
            nc.vector.tensor_copy(dst, win.indirect(lists[tab][:, 32 * b0 : 32 * b1]))

        def quant(src, name, fmt, slot=None):
            codes = held([P, N], U32, "c_" + name, slot)
            scales = held([P, N], U8, "s_" + name)
            nc.vector.quantize_mx(out=codes[:].bitcast(fmt), scales=scales[:], in_=src[:])
            return codes, scales, fmt

        def mm(out, lhs, blk, rhs):
            cols = slice(P * blk, P * (blk + 1))
            nc.tensor.matmul_mx(out=out, lhsT=lhs[0][:, cols].bitcast(lhs[2]), lhsT_scale=lhs[1][:, cols],
                                rhs=rhs[0][:].bitcast(rhs[2]), rhs_scale=rhs[1][:], start=True, stop=True)

        def weave(tab, b, fours, slot=None):
            q = held([P, 4 * N], BF16, "q_%s%d" % (tab, b), slot)
            lo, hi = place[tab, 0, b], place[tab, 1, b]
            src = gath[tab][:].rearrange("p (g c) -> p g c", c=2 * N)[:, lo : hi + 1 : hi - lo, :]
            if fours:
                nc.vector.tensor_copy(q[:].rearrange("p (t s u e) -> p s t u e", t=4, u=2, e=2), src.rearrange("p u (s t e) -> p s t u e", t=4, e=2))
            else:
                nc.vector.tensor_copy(q[:].rearrange("p (c u e) -> p c u e", u=2, e=2), src.rearrange("p u (c e) -> p c u e", e=2))
            return q

        def turned(name, words, banks, slot=None):
            dst = held([P, 4 * N], BF16, name, slot) if slot else turn.tile([P, 4 * N], BF16, name=name, tag="turn", align_bytes=64)
            for u, which in enumerate(banks):
                turn_pair(dst, words, u, which)
            return dst

        def turn_pair(dst, words, u, which):
            bank = new_bank(which)
            for t in range(4):
                nc.tensor.transpose(bank[:, t, :], words(u, t), ident[:])
            nc.scalar.copy(dst[:, 1024 * u : 1024 * (u + 1)].rearrange("q (e p t) -> q e p t", e=2, t=4),
                           bank[:].rearrange("q t p -> q (t p)").bitcast(BF16).rearrange("q (t p e) -> q e p t", t=4, e=2))

        def woven_words(q):
            return lambda u, t: q[:].bitcast(F32)[:, 256 * t + u : 256 * (t + 1) : 2]

        def gathered_words(u, t):
            return gath["v"][:].bitcast(F32)[:, N * place["v", u, 0] + t : N * (place["v", u, 0] + 1) : 4]

        def turn_h(h, dst, t):
            bank = new_bank("A" if t == 1 else "B")
            for j in range(2):
                for u in range(2):
                    nc.tensor.transpose(bank[:, 2 * j + u, :], h[:, t - 1 + j, :].bitcast(F32)[:, u:256:2], ident[:])
            nc.scalar.copy(dst[:].bitcast(F32).rearrange("q (s t u) -> q s t u", t=4, u=2)[:, :, t - 1 : t + 1, :],
                           bank[:].rearrange("q (j u) s -> q s j u", u=2))

        def weave_h(h, name):
            hq = held([P, 4 * N], BF16, name, "hx")
            for k in range(4):
                nc.scalar.copy(hq[:, N * k : N * (k + 1)].rearrange("p (c j t) -> p c t j", j=4, t=4),
                               h[:, :, P * k : P * (k + 1)].rearrange("p t (c j) -> p c t j", j=4))
            return hq

        def flat(bank):
            return bank[:].rearrange("p k s -> p (k s)")

        def product(res, lhs, blk, rhs, which="r"):
            acc = new_bank(which)
            mm(flat(acc), lhs, blk, rhs)
            nc.scalar.copy(res[:, blk, :], flat(acc))

        def scatter(win, tab, b, src):
            nc.vector.tensor_copy(win[:].indirect(lists[tab][:, 32 * b : 32 * (b + 1)]), src)

        ts_row = turn.tile([P, B * N], F32, name="ts_row", tag="turn", align_bytes=64)
        nc.vector.tensor_copy(ts_row[:], ts_win[:].indirect(lists["v"][:]))
        win_u = [window(k) for k in range(4)]
        win_v = [window(4)]

        cast(0, 513)
        cast(1, 1024)
        gather("u", 0, 0, 2)
        cast(2, 1024)
        cast(3, 1024)
        gather("u", 1, 0, 2)

        ts_col = keep.tile([P, 8], F32, name="ts_col")
        ts_all = keep.tile([P, N], F32, name="ts_all")
        bank = new_bank("A")
        for k in range(4):
            nc.tensor.transpose(bank[:, k, :], ts_row[:, P * k : P * (k + 1)], ident[:])
        nc.vector.tensor_copy(ts_col[:, 0:4], bank[:, :, 0])
        bank = new_bank("B")
        for k in range(4):
            nc.tensor.transpose(bank[:, k, :], ts_row[:, N + k : 2 * N : 4], ident[:])
        nc.vector.tensor_copy(ts_col[:, 4:8], bank[:, :, 0])
        bank = new_bank("A")
        for k in range(4):
            nc.tensor.transpose(bank[:, k, :], ts_col[:, k : k + 1].to_broadcast([P, P]), ident[:])
        nc.vector.tensor_copy(ts_all[:], flat(bank))

        qx0 = weave("u", 0, True)
        qx1 = weave("u", 1, True)
        xd0 = quant(qx0, "xd0", E4)
        xd1 = quant(qx1, "xd1", E4)
        cast(4, 1024)
        cast(5, 1024)
        gather("v", 0, 0, 2)
        cast(6, 1024)
        cast(7, 512)
        cast(8, 0)
        gather("v", 1, 0, 1)
        qw0 = weave("v", 0, False)
        wd0 = quant(qw0, "wd0", E4)
        wt0s = turned("wt0", gathered_words, "A")

        h0 = held([P, 4, N], BF16, "h0")
        ht0s = held([P, 4 * N], BF16, "ht0", "hx")
        e0 = []
        for t in range(4):
            a = new_bank("r")
            mm(flat(a), xd0, t, wd0)
            e0.append(held([P, N], F32, "e%d" % t))
            arg = held([P, N], F32, "arg") if t == 3 else e0[t]
            nc.vector.tensor_tensor(arg[:], flat(a), ts_all[:], MULT)
            nc.scalar.activation(e0[t][:], arg[:], EXP, scale=us_sb[:, 0, t : t + 1])
        for t in range(4):
            nc.vector.tensor_tensor(y_sb[0][:, t, :], e0[t][:], y_sb[0][:, t, :], SUB)
            if t % 2 == 1:
                for j in (t - 1, t):
                    nc.vector.scalar_tensor_tensor(h0[:, j, :], y_sb[0][:, j, :], us_sb[:, 0, j : j + 1], ts_all[:], MULT, MULT)
                turn_h(h0, ht0s, t)
        turn_pair(wt0s, gathered_words, 1, "r")
        xt0s = turned("xt0", woven_words(qx0), "CD")
        xt1s = turned("xt1", woven_words(qx1), "rr", "arg")
        wt0 = quant(wt0s, "wt0", E4, "e1")
        ht0 = quant(ht0s, "ht0", E5)
        du0 = held([P, 4, N], F32, "du0", "pair_u0")
        product(du0, wt0, 0, ht0)
        hq0s = weave_h(h0, "hq0")
        for t in range(1, 4):
            product(du0, wt0, t, ht0)
        gather("v", 1, 1, 2)
        win_v.extend(window(5 + k, slot) for k, slot in enumerate(("q_v0", "c_wd0", "e0")))
        qw1 = weave("v", 1, True, "e3")
        wd1 = quant(qw1, "wd1", E4)
        xt0 = quant(xt0s, "xt0", E4, "e2")
        xt1 = quant(xt1s, "xt1", E4)
        hq0 = quant(hq0s, "hq0", E5)

        h1 = held([P, 4, N], BF16, "h1")
        bt = held([P, 4, N], F32, "bt", "s2")
        e1 = held([P, 4, N], F32, "e_1", "s3")
        ny = held([P, 4, N], F32, "ny", "s0")
        for t in range(4):
            a = new_bank("r")
            mm(flat(a), wd1, t, xd1)
            nc.scalar.activation(bt[:, t, :], flat(a), COPY, scale=ts_col[:, 4 + t : 5 + t])
        dv0 = held([P, 4, N], F32, "dv0", "pair_u1")
        for t in range(3):
            product(dv0, xt0, t, hq0)
        for t in range(4):
            bank = new_bank("AB"[t % 2])
            for k in range(4):
                nc.tensor.transpose(bank[:, k, :], bt[:, k, P * t : P * (t + 1)], ident[:])
            usc = us_sb[:, 1, t : t + 1]
            nc.scalar.activation(e1[:, t, :], flat(bank), EXP, scale=usc)
            nc.scalar.activation(e1[:, t, :], e1[:, t, :], COPY, scale=usc)
            nc.scalar.activation(ny[:, t, :].rearrange("p (k s) -> p s k", k=4), y_sb[1][:, t, :].rearrange("p (s k) -> p s k", k=4), COPY, scale=nus[:, t : t + 1])
        hq1s = held([P, 4 * N], BF16, "hq1", "hx")
        for k in range(4):
            bank = new_bank("CD"[k % 2])
            for t in range(4):
                nc.tensor.matmul(bank[:, t, :], e1[:, t, P * k : P * (k + 1)], ident[:], start=True, stop=False, is_transpose=True)
                nc.tensor.matmul(bank[:, t, :], ny[:, t, P * k : P * (k + 1)], ident[:], start=False, stop=True, is_transpose=True)
            nc.scalar.activation(h1[:, k, :].rearrange("p (s t) -> p s t", t=4), bank[:].rearrange("p t s -> p s t"), COPY,
                                 scale=ts_col[:, 4 + k : 5 + k])
            if k % 2 == 1:
                turn_h(h1, hq1s, k)
        hq1 = quant(hq1s, "hq1", E5)
        product(dv0, xt0, 3, hq0, "B")
        dv1 = held([P, 4, N], F32, "dv1", "pair_u0")
        for t in range(2):
            product(dv1, xt1, t, hq1)
        ht1s = weave_h(h1, "ht1")
        wt1s = turned("wt1", woven_words(qw1), "CD")
        for t in range(2, 4):
            product(dv1, xt1, t, hq1)
        wt1 = quant(wt1s, "wt1", E4)
        ht1 = quant(ht1s, "ht1", E5)
        du1 = held([P, 4, N], F32, "du1", "pair_u1")
        for t in range(4):
            product(du1, wt1, t, ht1)

        out_v = out_0.rearrange("(p t) c -> p t c", t=4)
        out_u = out_1.rearrange("(p t) c -> p t c", t=4)
        for t in range(4):
            scatter(win_u[t], "u", 0, du0[:, t, :])
        for t in range(4):
            scatter(win_v[t], "v", 0, dv0[:, t, :])
        for t in range(4):
            scatter(win_v[t], "v", 1, dv1[:, t, :])
            nc.sync.dma_start(out_v[:, t, :], win_v[t][:])
        for t in range(4):
            scatter(win_u[t], "u", 1, du1[:, t, :])
            nc.sync.dma_start(out_u[:, t, :], win_u[t][:])
